import numpy as np
import ml_dtypes


def mxq(x, axis, fmt="e4m3"):
    dtype, down = {"e4m3": (ml_dtypes.float8_e4m3fn, 7), "e5m2": (ml_dtypes.float8_e5m2, 14)}[fmt]
    v = np.moveaxis(np.asarray(x, np.float32).astype(ml_dtypes.bfloat16).astype(np.float64), axis, -1)
    blocks = v.reshape(v.shape[:-1] + (-1, 32))
    amax = np.abs(blocks).max(-1, keepdims=True)
    byte = np.maximum(np.where(amax > 0, np.frexp(amax)[1] - 1 + 127, 0) - down, 1)
    scale = np.exp2(byte - 127.0)
    codes = (blocks / scale).astype(np.float32).astype(dtype).astype(np.float64)
    return np.moveaxis((codes * scale).reshape(v.shape), -1, axis)


WIDE = False


def mx_kscale(k):
    if not WIDE:
        return np.ones(k)
    levels = np.array([10, -10, 5, -5, 0])
    if k % 512:
        return np.exp2(np.random.permutation(np.resize(levels, k // 32))).repeat(32)
    a = np.empty((k // 512, 16))
    for p in range(k // 512):
        a[p, :8] = np.random.permutation(np.resize(levels, 8))
        for g in range(8):
            far = levels[np.abs(levels - a[p, g]) >= 10]
            a[p, g + 8] = far[np.random.randint(len(far))]
    return np.exp2(a.ravel()).repeat(32)


def f64(x):
    return np.asarray(x).astype(np.float64)


def striped(idx):
    return np.tile(idx.reshape(-1, 16).T, (8, 1)).astype(np.uint16)


def unstriped(offs):
    return offs[:16].T.reshape(-1).astype(np.int64)


K, T, S, N = 1024, 512, 512, 2048


def setup_inputs():
    n = np.random.standard_normal
    s = mx_kscale(K)[:, None]
    return {
        "w": (n((K, N)) / np.sqrt(K) / s).astype(np.float32),
        "xT": (n((K, T)) * s).astype(np.float32),
        "b": (0.3 * n((S, 1))).astype(np.float32),
        "offs": striped(np.sort(np.random.permutation(N)[:S])),
    }


def reference(w, xT, b, offs):
    idx = unstriped(offs)
    wq = mxq(f64(w)[:, idx], 0, "e4m3")
    return (wq.T @ mxq(f64(xT), 0, "e4m3")) + f64(b)

from contextlib import ExitStack

import concourse.mybir as mybir
from concourse.masks import make_identity

K, N, S, T = 1024, 2048, 512, 512
FLOPS = 2 * K * S * T

F32 = mybir.dt.float32
BF16 = mybir.dt.bfloat16
U32 = mybir.dt.uint32
U16 = mybir.dt.uint16
U8 = mybir.dt.uint8
FP8X4 = mybir.dt.float8_e4m3fn_x4
IDENTITY = mybir.ActivationFunctionType.Identity

P = 128
PACK = 4
K_PASS = P * PACK
PASSES = K // K_PASS
BLOCKS = S // P
HALF = 256
OFFS_PER_COLUMN = 16
SPLIT = 168


def tile_picked_neuron_lin_bias_srt_e_kernel(tc, w, xT, b, offs, out):
    nc = tc.nc
    with ExitStack() as ctx:
        keep = ctx.enter_context(tc.tile_pool(name="keep", bufs=1))
        psum = ctx.enter_context(tc.psum_pool(name="psum", bufs=1))

        offsets = keep.tile([P, S // OFFS_PER_COLUMN], U16, name="offsets")
        w_raw = [keep.tile([P, PACK, N], F32, name="w_raw%d" % a) for a in range(PASSES)]
        x_raw = [[keep.tile([P, PACK, HALF], F32, name="x_raw%d%d" % (a, h)) for h in range(2)] for a in range(PASSES)]
        w_grp = [keep.tile([P, S, PACK], BF16, name="w_grp%d" % a, align_bytes=64) for a in range(PASSES)]
        x_grp = [[keep.tile([P, HALF, PACK], BF16, name="x_grp%d%d" % (a, h), align_bytes=64) for h in range(2)] for a in range(PASSES)]
        w_codes = [keep.tile([P, S], U32, name="w_codes%d" % a, align_bytes=64) for a in range(PASSES)]
        w_scales = [keep.tile([P, S], U8, name="w_scales%d" % a, align_bytes=64) for a in range(PASSES)]
        x_codes = [[keep.tile([P, HALF], U32, name="x_codes%d%d" % (a, h), align_bytes=64) for h in range(2)] for a in range(PASSES)]
        x_scales = [[keep.tile([P, HALF], U8, name="x_scales%d%d" % (a, h), align_bytes=64) for h in range(2)] for a in range(PASSES)]
        result = [[keep.tile([P, 2, HALF], F32, name="result%d%d" % (h, q)) for q in range(BLOCKS // 2)] for h in range(2)]
        b_rows = keep.tile([P, P], F32, name="b_rows")
        ident = keep.tile([P, P], F32, name="ident")
        bias = keep.tile([P, BLOCKS], F32, name="bias")

        w_view = [w[a * K_PASS : (a + 1) * K_PASS, :].rearrange("(p j) n -> p j n", j=PACK) for a in range(PASSES)]
        x_view = [xT[a * K_PASS : (a + 1) * K_PASS, :].rearrange("(p j) t -> p j t", j=PACK) for a in range(PASSES)]
        out_view = out.rearrange("(m p) t -> p m t", p=P)

        def load_w(a, j0, j1):
            nc.sync.dma_start(out=w_raw[a][:, j0:j1, :], in_=w_view[a][:, j0:j1, :])

        def load_x(a, h):
            nc.sync.dma_start(out=x_raw[a][h][:], in_=x_view[a][:, :, h * HALF : (h + 1) * HALF])

        load_w(0, 0, 2)
        nc.sync.dma_start(offsets[:], offs)
        load_w(0, 2, 4)
        load_w(1, 0, 2)
        load_x(0, 0)
        load_w(1, 2, 3)
        load_w(1, 3, 4)
        load_x(1, 0)
        load_x(0, 1)
        load_x(1, 1)

        nc.gpsimd.memset(b_rows[:], 0.0)
        make_identity(nc, ident[:])
        nc.scalar.dma_start(out=b_rows[0:BLOCKS, :], in_=b.rearrange("(m p) o -> m (p o)", p=P))
        b_bank = psum.tile([P, 512], F32, name="bank7")
        nc.tensor.transpose(b_bank[:, 0:P], b_rows[:], ident[:])
        nc.scalar.copy(bias[:], b_bank[:, 0:BLOCKS])

        def gather(a, j, lo, hi):
            nc.vector.tensor_copy(
                w_grp[a][:, lo:hi, j],
                w_raw[a][:, j, :].indirect(offsets[:, lo // OFFS_PER_COLUMN : hi // OFFS_PER_COLUMN]),
            )

        def quantize_w(a, lo, hi):
            nc.vector.quantize_mx(
                out=w_codes[a][:, lo:hi].bitcast(FP8X4),
                scales=w_scales[a][:, lo:hi],
                in_=w_grp[a][:, lo:hi, :].rearrange("p s j -> p (s j)"),
            )

        def interleave_scalar(a, h, lo, hi):
            nc.scalar.copy(x_grp[a][h][:, lo:hi, :], x_raw[a][h][:, :, lo:hi].rearrange("p j t -> p t j"))

        def interleave_vector(a, h, lo, hi):
            nc.vector.tensor_copy(x_grp[a][h][:, lo:hi, :], x_raw[a][h][:, :, lo:hi].rearrange("p j t -> p t j"))

        def quantize_x(a, h):
            nc.vector.quantize_mx(
                out=x_codes[a][h][:].bitcast(FP8X4),
                scales=x_scales[a][h][:],
                in_=x_grp[a][h][:].rearrange("p t j -> p (t j)"),
            )

        def multiply(a, m, h):
            cols = slice(m * P, (m + 1) * P)
            nc.tensor.matmul_mx(
                out=banks[h][m][:, 0:HALF],
                lhsT=w_codes[a][:, cols].bitcast(FP8X4),
                lhsT_scale=w_scales[a][:, cols],
                rhs=x_codes[a][h][:].bitcast(FP8X4),
                rhs_scale=x_scales[a][h][:],
                start=(a == 0),
                stop=(a == PASSES - 1),
            )

        def finish(m, h):
            dst = result[h][m // 2][:, m % 2, :]
            src = banks[h][m][:, 0:HALF]
            if m % 2 == 0:
                nc.scalar.activation(dst, src, IDENTITY, bias=bias[:, m : m + 1])
            else:
                nc.vector.tensor_scalar_add(dst, src, bias[:, m : m + 1])
                nc.sync.dma_start(out=out_view[:, m - 1 : m + 1, h * HALF : (h + 1) * HALF], in_=result[h][m // 2][:])

        banks = [[psum.tile([P, 512], F32, name="bank%d" % (h * BLOCKS + m)) for m in range(BLOCKS)] for h in range(2)]

        for j in range(PACK):
            gather(0, j, 0, S)
        quantize_w(0, 0, S)
        for j in range(2):
            gather(1, j, 0, S)
        interleave_scalar(0, 0, 0, HALF)
        quantize_x(0, 0)
        for m in range(BLOCKS):
            multiply(0, m, 0)
        gather(1, 2, 0, S)
        gather(1, 3, 0, HALF)
        gather(1, 3, HALF, S)
        quantize_w(1, 0, HALF)
        quantize_w(1, HALF, S)
        interleave_scalar(1, 0, 0, HALF)
        quantize_x(1, 0)
        for m in range(BLOCKS):
            multiply(1, m, 0)
            finish(m, 0)
        interleave_vector(0, 1, 0, SPLIT)
        interleave_scalar(0, 1, SPLIT, HALF)
        quantize_x(0, 1)
        for m in range(BLOCKS):
            multiply(0, m, 1)
        interleave_vector(1, 1, 0, SPLIT)
        interleave_scalar(1, 1, SPLIT, HALF)
        quantize_x(1, 1)
        for m in range(BLOCKS):
            multiply(1, m, 1)
            finish(m, 1)
